import numpy as np
import ml_dtypes


def mxq(x, axis, fmt="e4m3"):
    dtype, down = {"e4m3": (ml_dtypes.float8_e4m3fn, 7), "e5m2": (ml_dtypes.float8_e5m2, 14)}[fmt]
    v = np.moveaxis(np.asarray(x, np.float32).astype(ml_dtypes.bfloat16).astype(np.float64), axis, -1)
    blocks = v.reshape(v.shape[:-1] + (-1, 32))
    amax = np.abs(blocks).max(-1, keepdims=True)
    byte = np.maximum(np.where(amax > 0, np.frexp(amax)[1] - 1 + 127, 0) - down, 1)
    scale = np.exp2(byte - 127.0)
    codes = (blocks / scale).astype(np.float32).astype(dtype).astype(np.float64)
    return np.moveaxis((codes * scale).reshape(v.shape), -1, axis)


WIDE = False


def mx_kscale(k):
    if not WIDE:
        return np.ones(k)
    levels = np.array([10, -10, 5, -5, 0])
    if k % 512:
        return np.exp2(np.random.permutation(np.resize(levels, k // 32))).repeat(32)
    a = np.empty((k // 512, 16))
    for p in range(k // 512):
        a[p, :8] = np.random.permutation(np.resize(levels, 8))
        for g in range(8):
            far = levels[np.abs(levels - a[p, g]) >= 10]
            a[p, g + 8] = far[np.random.randint(len(far))]
    return np.exp2(a.ravel()).repeat(32)


def f64(x):
    return np.asarray(x).astype(np.float64)


def striped8(idx):
    return np.concatenate([v.reshape(-1, 16).T for v in idx]).astype(np.uint16)


def unstriped8(offs):
    return np.stack([offs[16 * g:16 * g + 16].T.reshape(-1) for g in range(8)]).astype(np.int64)


K, M, T, S = 1536, 256, 1024, 512


def setup_inputs():
    n = np.random.standard_normal
    s = mx_kscale(K)[:, None]
    return {
        "xT": (n((K, T)) * s).astype(np.float32),
        "w": (n((K, M)) / np.sqrt(K) / s).astype(np.float32),
        "wgt": np.repeat(np.random.uniform(0.5, 2.0, (8, S)), 16, axis=0).astype(np.float32),
        "b": (0.3 * n(256)).astype(np.float32),
        "wgo": np.repeat(np.random.uniform(0.5, 2.0, (8, S)), 16, axis=0).astype(np.float32),
        "offs": striped8(np.stack([np.random.permutation(T)[:S] for _ in range(8)])),
        "offs2": striped8(np.stack([np.random.permutation(T)[:S] for _ in range(8)])),
    }


def reference(xT, w, wgt, b, wgo, offs, offs2):
    idx = unstriped8(offs)
    group = np.arange(K) % 512 // 64
    xg = f64(wgt)[np.arange(K) // 4 % 128] * f64(xT)[np.arange(K)[:, None], idx[group]]
    xT_ = mxq(xg, 0, "e4m3")
    w_ = mxq(f64(w), 0, "e4m3")
    y = w_.T @ xT_
    place = unstriped8(offs2)[np.arange(M) % 128 // 16]
    out = np.zeros((M, T))
    out[np.arange(M)[:, None], place] = f64(wgo)[np.arange(M) % 128] * (y + f64(b)[:, None])
    return out

@@ -1,0 +1,218 @@
+import concourse.mybir as mybir
+
+K, M, T, S = 1536, 256, 1024, 512
+
+F32 = mybir.dt.float32
+BF16 = mybir.dt.bfloat16
+U32 = mybir.dt.uint32
+U16 = mybir.dt.uint16
+U8 = mybir.dt.uint8
+FP8X4 = mybir.dt.float8_e4m3fn_x4
+MULT = mybir.AluOpType.mult
+IDENTITY = mybir.ActivationFunctionType.Identity
+
+P = 128
+PACK = 4
+K_PASS = P * PACK
+PASSES = K // K_PASS
+LAST = PASSES - 1
+M_TILES = M // P
+HALVES = 2
+H = S // HALVES
+HCOLS = H // 16
+
+FLOPS = 2 * K * M * S
+
+
+def tile_list_hboth_bias_kernel(tc, xT, w, wgt, b, wgo, offs, offs2, out):
+    nc = tc.nc
+
+    with (
+        tc.tile_pool(name="keep", bufs=1) as keep,
+        tc.psum_pool(name="psum", bufs=1) as psum,
+    ):
+        idx = keep.tile([P, S // 16], U16, name="idx")
+        idx2 = keep.tile([P, S // 16], U16, name="idx2")
+        wgt_sb = [keep.tile([P, H], F32, name=f"wgt{h}") for h in range(HALVES)]
+        wgo_sb = keep.tile([P, S], F32, name="wgo_sb")
+        b_sb = [keep.tile([P, 1], F32, name=f"b{m}") for m in range(M_TILES)]
+        x_sb = [[keep.tile([P, T], F32, name=f"x{a}_{i}") for i in range(PACK)] for a in range(PASSES)]
+        w_sb = [keep.tile([P, PACK, M], F32, name=f"w{a}") for a in range(PASSES)]
+
+        def load_x(a, i):
+            rows = xT[a * K_PASS : (a + 1) * K_PASS, :].rearrange("(p i) t -> p i t", i=PACK)
+            nc.sync.dma_start(out=x_sb[a][i][:], in_=rows[:, i, :])
+
+        def load_w(a):
+            rows = w[a * K_PASS : (a + 1) * K_PASS, :].rearrange("(p i) n -> p i n", i=PACK)
+            nc.sync.dma_start(out=w_sb[a][:], in_=rows)
+
+        nc.sync.dma_start(out=idx[:], in_=offs)
+        nc.sync.dma_start(out=wgt_sb[0][:], in_=wgt[:, 0:H])
+        load_x(0, 0)
+        nc.sync.dma_start(out=wgt_sb[1][:], in_=wgt[:, H:S])
+        load_x(0, 1)
+        load_x(0, 2)
+        load_x(0, 3)
+        load_x(1, 0)
+        load_x(1, 1)
+        load_w(0)
+        load_x(1, 2)
+        load_x(1, 3)
+        load_x(2, 0)
+        load_w(1)
+        load_x(2, 1)
+        load_x(2, 2)
+        load_w(2)
+        load_x(2, 3)
+        nc.sync.dma_start(out=idx2[:], in_=offs2)
+        nc.sync.dma_start(out=wgo_sb[:], in_=wgo)
+        for m in range(M_TILES):
+            nc.sync.dma_start(out=b_sb[m][:], in_=b[m * P : (m + 1) * P].rearrange("(p o) -> p o", o=1))
+
+        placed = [keep.tile([P, T], F32, name=f"placed{m}") for m in range(M_TILES)]
+        for m in range(M_TILES):
+            nc.vector.memset(placed[m][:], 0.0)
+
+        held = {"xbf2_0": "late", "g2_384": "late", "y1_0": "late"}
+
+        def new_tile(shape, dtype, name):
+            return keep.tile(shape, dtype, name=name, tag=held.get(name, name), align_bytes=64)
+
+        g_sb = {}
+        w_bf = {}
+        w_codes = [keep.tile([P, M], U32, name=f"wc{a}", align_bytes=64) for a in range(PASSES)]
+        w_scales = [keep.tile([P, M], U8, name=f"ws{a}", align_bytes=64) for a in range(PASSES)]
+        acc = [[psum.tile([P, H], F32, name=f"acc{m}_{h}") for h in range(HALVES)] for m in range(M_TILES)]
+        y_sb = {}
+
+        def gather(a, i, lo, hi):
+            if (a, lo) not in g_sb:
+                g_sb[a, lo] = new_tile([P, PACK, hi - lo], F32, f"g{a}_{lo}")
+            nc.vector.tensor_tensor(
+                g_sb[a, lo][:, i, :],
+                x_sb[a][i][:].indirect(idx[:, lo // 16 : hi // 16]),
+                wgt_sb[lo // H][:, lo % H : lo % H + hi - lo],
+                MULT,
+            )
+
+        x_bf, x_codes, x_scales = {}, {}, {}
+
+        def interleave_x(a, lo, hi, vector_from=None):
+            mid = hi if vector_from is None else vector_from
+            x_bf[a, lo] = new_tile([P, hi - lo, PACK], BF16, f"xbf{a}_{lo}")
+            for copy, c0, c1 in ((nc.scalar.copy, lo, mid), (nc.vector.tensor_copy, mid, hi)):
+                if c0 < c1:
+                    copy(
+                        out=x_bf[a, lo][:, c0 - lo : c1 - lo, :],
+                        in_=g_sb[a, lo][:, :, c0 - lo : c1 - lo].rearrange("p i j -> p j i"),
+                    )
+
+        def quantize_x(a, lo, hi):
+            h = lo // H
+            if (a, h) not in x_codes:
+                x_codes[a, h] = new_tile([P, H], U32, f"xc{a}_{h}")
+                x_scales[a, h] = new_tile([P, H], U8, f"xs{a}_{h}")
+            js = slice(lo % H, lo % H + hi - lo)
+            nc.vector.quantize_mx(
+                out=x_codes[a, h][:, js].bitcast(FP8X4),
+                scales=x_scales[a, h][:, js],
+                in_=x_bf[a, lo][:].rearrange("p j i -> p (j i)"),
+            )
+
+        def interleave_w(a, lo=0, hi=M):
+            if a not in w_bf:
+                w_bf[a] = new_tile([P, M, PACK], BF16, f"wbf{a}")
+            nc.scalar.copy(out=w_bf[a][:, lo:hi, :], in_=w_sb[a][:, :, lo:hi].rearrange("p i n -> p n i"))
+
+        def quantize_w(a, lo=0, hi=M):
+            nc.vector.quantize_mx(
+                out=w_codes[a][:, lo:hi].bitcast(FP8X4),
+                scales=w_scales[a][:, lo:hi],
+                in_=w_bf[a][:].rearrange("p n i -> p (n i)")[:, PACK * lo : PACK * hi],
+            )
+
+        def multiply(a, m, h):
+            ns = slice(m * P, (m + 1) * P)
+            nc.tensor.matmul_mx(
+                out=acc[m][h][:],
+                lhsT=w_codes[a][:, ns].bitcast(FP8X4),
+                lhsT_scale=w_scales[a][:, ns],
+                rhs=x_codes[a, h][:].bitcast(FP8X4),
+                rhs_scale=x_scales[a, h][:],
+                start=(a == 0),
+                stop=(a == LAST),
+            )
+
+        def add_bias(m, h):
+            y_sb[m, h] = new_tile([P, H], F32, f"y{m}_{h}")
+            nc.scalar.activation(out=y_sb[m, h][:], in_=acc[m][h][:], func=IDENTITY, bias=b_sb[m][:])
+
+        def scatter(m, h):
+            nc.vector.tensor_tensor(
+                placed[m][:].indirect(idx2[:, h * HCOLS : (h + 1) * HCOLS]),
+                y_sb[m, h][:],
+                wgo_sb[:, h * H : (h + 1) * H],
+                MULT,
+            )
+
+        def multiply_pass(a):
+            for m in range(M_TILES):
+                for h in range(HALVES):
+                    multiply(a, m, h)
+
+        A, B, B1, B2 = (0, 256), (256, 512), (256, 384), (384, 512)
+        for i in range(PACK):
+            gather(0, i, *A)
+            gather(0, i, *B)
+        interleave_x(0, *A)
+        interleave_x(0, *B)
+        for i in range(2):
+            gather(1, i, *A)
+            gather(1, i, *B)
+        quantize_x(0, *A)
+        quantize_x(0, *B)
+        interleave_w(0)
+        for i in range(2, PACK):
+            gather(1, i, *A)
+            gather(1, i, *B)
+        interleave_x(1, *A)
+        interleave_x(1, *B)
+        quantize_w(0)
+        multiply_pass(0)
+
+        for i in range(2):
+            gather(2, i, *A)
+            gather(2, i, *B1)
+        interleave_w(1)
+        gather(2, 2, *A)
+        gather(2, 2, *B1)
+        quantize_x(1, *A)
+        quantize_x(1, *B)
+        interleave_w(2)
+        quantize_w(1)
+        multiply_pass(1)
+        gather(2, 3, *A)
+        interleave_x(2, *A, 128)
+        quantize_w(2)
+        gather(2, 3, *B1)
+        quantize_x(2, *A)
+        for m in range(M_TILES):
+            multiply(2, m, 0)
+        add_bias(0, 0)
+        interleave_x(2, *B1)
+        for i in range(PACK):
+            gather(2, i, *B2)
+        interleave_x(2, *B2)
+        scatter(0, 0)
+        add_bias(1, 0)
+        quantize_x(2, *B1)
+        quantize_x(2, *B2)
+        for m in range(M_TILES):
+            multiply(2, m, 1)
+        scatter(1, 0)
+        for m in range(M_TILES):
+            add_bias(m, 1)
+        for m in range(M_TILES):
+            scatter(m, 1)
+            nc.sync.dma_start(out=out[m * P : (m + 1) * P, :], in_=placed[m][:])

@@ -17,9 +17,8 @@ K_PASS = P * PACK
 PASSES = K // K_PASS
 LAST = PASSES - 1
 M_TILES = M // P
-HALVES = 2
-H = S // HALVES
-HCOLS = H // 16
+H = S // 2
+RUN = 4
 
 FLOPS = 2 * K * M * S
 
@@ -31,188 +30,195 @@ def tile_list_hboth_bias_kernel(tc, xT, w, wgt, b, wgo, offs, offs2, out):
         tc.tile_pool(name="keep", bufs=1) as keep,
         tc.psum_pool(name="psum", bufs=1) as psum,
     ):
+        held = {
+            "wbf2_0": "late",
+            "g2_384": "late",
+            "y1_0": "late",
+            "xbf2_0": "parts",
+            "xbf2_256": "parts",
+            "xbf2_384": "parts",
+        }
+
+        def new_tile(shape, dtype, name):
+            return keep.tile(shape, dtype, name=name, tag=held.get(name, name), align_bytes=64)
+
+        WHOLE, A, B = (0, S), (0, H), (H, S)
+        A1, A2, B1, B2 = (0, 128), (128, 256), (256, 384), (384, 512)
+        FRONT = (0, 384)
+        ALL_N, N0, N1 = (0, M), (0, P), (P, M)
+
         idx = keep.tile([P, S // 16], U16, name="idx")
         idx2 = keep.tile([P, S // 16], U16, name="idx2")
-        wgt_sb = [keep.tile([P, H], F32, name=f"wgt{h}") for h in range(HALVES)]
-        wgo_sb = keep.tile([P, S], F32, name="wgo_sb")
-        b_sb = [keep.tile([P, 1], F32, name=f"b{m}") for m in range(M_TILES)]
-        x_sb = [[keep.tile([P, T], F32, name=f"x{a}_{i}") for i in range(PACK)] for a in range(PASSES)]
-        w_sb = [keep.tile([P, PACK, M], F32, name=f"w{a}") for a in range(PASSES)]
+        wgt_sb = new_tile([P, S], F32, "wgt_sb")
+        wgo_sb = new_tile([P, S], F32, "wgo_sb")
+        b_sb = [new_tile([P, 1], F32, f"b{m}") for m in range(M_TILES)]
+        x_sb = [[new_tile([P, T], F32, f"x{a}_{i}") for i in range(PACK)] for a in range(PASSES)]
+        w_sb = {}
 
         def load_x(a, i):
             rows = xT[a * K_PASS : (a + 1) * K_PASS, :].rearrange("(p i) t -> p i t", i=PACK)
             nc.sync.dma_start(out=x_sb[a][i][:], in_=rows[:, i, :])
 
-        def load_w(a):
-            rows = w[a * K_PASS : (a + 1) * K_PASS, :].rearrange("(p i) n -> p i n", i=PACK)
-            nc.sync.dma_start(out=w_sb[a][:], in_=rows)
+        def load_w(a, ns):
+            w_sb[a, ns] = new_tile([P, PACK, ns[1] - ns[0]], F32, f"w{a}_{ns[0]}")
+            rows = w[a * K_PASS : (a + 1) * K_PASS, ns[0] : ns[1]].rearrange("(p i) n -> p i n", i=PACK)
+            nc.sync.dma_start(out=w_sb[a, ns][:], in_=rows)
+
+        def load_b(m):
+            nc.sync.dma_start(out=b_sb[m][:], in_=b[m * P : (m + 1) * P].rearrange("(p o) -> p o", o=1))
 
         nc.sync.dma_start(out=idx[:], in_=offs)
-        nc.sync.dma_start(out=wgt_sb[0][:], in_=wgt[:, 0:H])
+        nc.sync.dma_start(out=wgt_sb[:, 0:H], in_=wgt[:, 0:H])
         load_x(0, 0)
-        nc.sync.dma_start(out=wgt_sb[1][:], in_=wgt[:, H:S])
-        load_x(0, 1)
-        load_x(0, 2)
-        load_x(0, 3)
+        nc.sync.dma_start(out=wgt_sb[:, H:S], in_=wgt[:, H:S])
+        for i in range(1, PACK):
+            load_x(0, i)
         load_x(1, 0)
         load_x(1, 1)
-        load_w(0)
+        load_w(0, ALL_N)
         load_x(1, 2)
         load_x(1, 3)
         load_x(2, 0)
-        load_w(1)
         load_x(2, 1)
+        load_w(1, ALL_N)
         load_x(2, 2)
-        load_w(2)
         load_x(2, 3)
+        load_w(2, ALL_N)
+        load_b(0)
         nc.sync.dma_start(out=idx2[:], in_=offs2)
         nc.sync.dma_start(out=wgo_sb[:], in_=wgo)
-        for m in range(M_TILES):
-            nc.sync.dma_start(out=b_sb[m][:], in_=b[m * P : (m + 1) * P].rearrange("(p o) -> p o", o=1))
+        load_b(1)
 
-        placed = [keep.tile([P, T], F32, name=f"placed{m}") for m in range(M_TILES)]
+        placed = [new_tile([P, T], F32, f"placed{m}") for m in range(M_TILES)]
         for m in range(M_TILES):
             nc.vector.memset(placed[m][:], 0.0)
 
-        held = {"xbf2_0": "late", "g2_384": "late", "y1_0": "late"}
+        g_sb, x_bf, w_bf, acc, y_sb = {}, {}, {}, {}, {}
+        x_codes = [new_tile([P, S], U32, f"xc{a}") for a in range(PASSES)]
+        x_scales = [new_tile([P, S], U8, f"xs{a}") for a in range(PASSES)]
+        w_codes = [new_tile([P, M], U32, f"wc{a}") for a in range(PASSES)]
+        w_scales = [new_tile([P, M], U8, f"ws{a}") for a in range(PASSES)]
 
-        def new_tile(shape, dtype, name):
-            return keep.tile(shape, dtype, name=name, tag=held.get(name, name), align_bytes=64)
+        def within(part, whole):
+            return slice(part[0] - whole[0], part[1] - whole[0])
 
-        g_sb = {}
-        w_bf = {}
-        w_codes = [keep.tile([P, M], U32, name=f"wc{a}", align_bytes=64) for a in range(PASSES)]
-        w_scales = [keep.tile([P, M], U8, name=f"ws{a}", align_bytes=64) for a in range(PASSES)]
-        acc = [[psum.tile([P, H], F32, name=f"acc{m}_{h}") for h in range(HALVES)] for m in range(M_TILES)]
-        y_sb = {}
-
-        def gather(a, i, lo, hi):
-            if (a, lo) not in g_sb:
-                g_sb[a, lo] = new_tile([P, PACK, hi - lo], F32, f"g{a}_{lo}")
+        def gather(a, i, part, into):
+            if (a, into) not in g_sb:
+                g_sb[a, into] = new_tile([P, PACK, into[1] - into[0]], F32, f"g{a}_{into[0]}")
             nc.vector.tensor_tensor(
-                g_sb[a, lo][:, i, :],
-                x_sb[a][i][:].indirect(idx[:, lo // 16 : hi // 16]),
-                wgt_sb[lo // H][:, lo % H : lo % H + hi - lo],
+                g_sb[a, into][:, i, within(part, into)],
+                x_sb[a][i][:].indirect(idx[:, part[0] // 16 : part[1] // 16]),
+                wgt_sb[:, part[0] : part[1]],
                 MULT,
             )
 
-        x_bf, x_codes, x_scales = {}, {}, {}
-
-        def interleave_x(a, lo, hi, vector_from=None):
-            mid = hi if vector_from is None else vector_from
-            x_bf[a, lo] = new_tile([P, hi - lo, PACK], BF16, f"xbf{a}_{lo}")
-            for copy, c0, c1 in ((nc.scalar.copy, lo, mid), (nc.vector.tensor_copy, mid, hi)):
-                if c0 < c1:
-                    copy(
-                        out=x_bf[a, lo][:, c0 - lo : c1 - lo, :],
-                        in_=g_sb[a, lo][:, :, c0 - lo : c1 - lo].rearrange("p i j -> p j i"),
-                    )
-
-        def quantize_x(a, lo, hi):
-            h = lo // H
-            if (a, h) not in x_codes:
-                x_codes[a, h] = new_tile([P, H], U32, f"xc{a}_{h}")
-                x_scales[a, h] = new_tile([P, H], U8, f"xs{a}_{h}")
-            js = slice(lo % H, lo % H + hi - lo)
-            nc.vector.quantize_mx(
-                out=x_codes[a, h][:, js].bitcast(FP8X4),
-                scales=x_scales[a, h][:, js],
-                in_=x_bf[a, lo][:].rearrange("p j i -> p (j i)"),
+        def weave(copy, dst, src):
+            copy(
+                out=dst.rearrange("p (c r) i -> p c i r", r=RUN),
+                in_=src.rearrange("p i (c r) -> p c i r", r=RUN),
             )
 
-        def interleave_w(a, lo=0, hi=M):
-            if a not in w_bf:
-                w_bf[a] = new_tile([P, M, PACK], BF16, f"wbf{a}")
-            nc.scalar.copy(out=w_bf[a][:, lo:hi, :], in_=w_sb[a][:, :, lo:hi].rearrange("p i n -> p n i"))
+        def interleave_x(a, part, source, into, copy):
+            if (a, into) not in x_bf:
+                x_bf[a, into] = new_tile([P, into[1] - into[0], PACK], BF16, f"xbf{a}_{into[0]}")
+            weave(copy, x_bf[a, into][:, within(part, into), :], g_sb[a, source][:, :, within(part, source)])
 
-        def quantize_w(a, lo=0, hi=M):
+        def quantize_x(a, part):
             nc.vector.quantize_mx(
-                out=w_codes[a][:, lo:hi].bitcast(FP8X4),
-                scales=w_scales[a][:, lo:hi],
-                in_=w_bf[a][:].rearrange("p n i -> p (n i)")[:, PACK * lo : PACK * hi],
+                out=x_codes[a][:, part[0] : part[1]].bitcast(FP8X4),
+                scales=x_scales[a][:, part[0] : part[1]],
+                in_=x_bf[a, part][:].rearrange("p j i -> p (j i)"),
             )
 
-        def multiply(a, m, h):
+        def interleave_w(a, ns):
+            w_bf[a, ns] = new_tile([P, ns[1] - ns[0], PACK], BF16, f"wbf{a}_{ns[0]}")
+            weave(nc.scalar.copy, w_bf[a, ns][:], w_sb[a, ALL_N][:, :, ns[0] : ns[1]])
+
+        def quantize_w(a, ns):
+            nc.vector.quantize_mx(
+                out=w_codes[a][:, ns[0] : ns[1]].bitcast(FP8X4),
+                scales=w_scales[a][:, ns[0] : ns[1]],
+                in_=w_bf[a, ns][:].rearrange("p n i -> p (n i)"),
+            )
+
+        def multiply(a, m, part):
+            if a == 0:
+                acc[m, part] = psum.tile([P, part[1] - part[0]], F32, name=f"acc{m}_{part[0]}")
             ns = slice(m * P, (m + 1) * P)
             nc.tensor.matmul_mx(
-                out=acc[m][h][:],
+                out=acc[m, part][:],
                 lhsT=w_codes[a][:, ns].bitcast(FP8X4),
                 lhsT_scale=w_scales[a][:, ns],
-                rhs=x_codes[a, h][:].bitcast(FP8X4),
-                rhs_scale=x_scales[a, h][:],
+                rhs=x_codes[a][:, part[0] : part[1]].bitcast(FP8X4),
+                rhs_scale=x_scales[a][:, part[0] : part[1]],
                 start=(a == 0),
                 stop=(a == LAST),
             )
 
-        def add_bias(m, h):
-            y_sb[m, h] = new_tile([P, H], F32, f"y{m}_{h}")
-            nc.scalar.activation(out=y_sb[m, h][:], in_=acc[m][h][:], func=IDENTITY, bias=b_sb[m][:])
+        def multiply_pass(a):
+            for part in (A, B):
+                for m in range(M_TILES):
+                    multiply(a, m, part)
 
-        def scatter(m, h):
+        def add_bias(m, part):
+            y_sb[m, part] = new_tile([P, part[1] - part[0]], F32, f"y{m}_{part[0]}")
+            nc.scalar.activation(out=y_sb[m, part][:], in_=acc[m, part][:], func=IDENTITY, bias=b_sb[m][:])
+
+        def scatter(m, part):
             nc.vector.tensor_tensor(
-                placed[m][:].indirect(idx2[:, h * HCOLS : (h + 1) * HCOLS]),
-                y_sb[m, h][:],
-                wgo_sb[:, h * H : (h + 1) * H],
+                placed[m][:].indirect(idx2[:, part[0] // 16 : part[1] // 16]),
+                y_sb[m, part][:],
+                wgo_sb[:, part[0] : part[1]],
                 MULT,
             )
 
-        def multiply_pass(a):
-            for m in range(M_TILES):
-                for h in range(HALVES):
-                    multiply(a, m, h)
-
-        A, B, B1, B2 = (0, 256), (256, 512), (256, 384), (384, 512)
-        for i in range(PACK):
-            gather(0, i, *A)
-            gather(0, i, *B)
-        interleave_x(0, *A)
-        interleave_x(0, *B)
+        gather(0, 0, A, WHOLE)
+        gather(0, 0, B, WHOLE)
+        for i in range(1, PACK):
+            gather(0, i, WHOLE, WHOLE)
+        interleave_x(0, WHOLE, WHOLE, WHOLE, nc.scalar.copy)
         for i in range(2):
-            gather(1, i, *A)
-            gather(1, i, *B)
-        quantize_x(0, *A)
-        quantize_x(0, *B)
-        interleave_w(0)
-        for i in range(2, PACK):
-            gather(1, i, *A)
-            gather(1, i, *B)
-        interleave_x(1, *A)
-        interleave_x(1, *B)
-        quantize_w(0)
+            gather(1, i, WHOLE, WHOLE)
+        quantize_x(0, WHOLE)
+        interleave_w(0, ALL_N)
+        gather(1, 2, WHOLE, WHOLE)
+        quantize_w(0, ALL_N)
         multiply_pass(0)
-
-        for i in range(2):
-            gather(2, i, *A)
-            gather(2, i, *B1)
-        interleave_w(1)
-        gather(2, 2, *A)
-        gather(2, 2, *B1)
-        quantize_x(1, *A)
-        quantize_x(1, *B)
-        interleave_w(2)
-        quantize_w(1)
+        for part in (A, B):
+            gather(1, 3, part, WHOLE)
+            interleave_x(1, part, WHOLE, part, nc.scalar.copy)
+        for i, part in enumerate((A, B)):
+            gather(LAST, i, FRONT, FRONT)
+            quantize_x(1, part)
+        interleave_w(1, ALL_N)
+        gather(LAST, 2, FRONT, FRONT)
+        quantize_w(1, ALL_N)
         multiply_pass(1)
-        gather(2, 3, *A)
-        interleave_x(2, *A, 128)
-        quantize_w(2)
-        gather(2, 3, *B1)
-        quantize_x(2, *A)
-        for m in range(M_TILES):
-            multiply(2, m, 0)
-        add_bias(0, 0)
-        interleave_x(2, *B1)
+        gather(LAST, 3, A, FRONT)
+        interleave_x(LAST, A1, FRONT, A, nc.scalar.copy)
+        gather(LAST, 3, B1, FRONT)
+        interleave_x(LAST, A2, FRONT, A, nc.vector.tensor_copy)
+        interleave_w(LAST, N0)
+        quantize_x(LAST, A)
+        quantize_w(LAST, N0)
+        multiply(LAST, 0, A)
+        interleave_w(LAST, N1)
+        interleave_x(LAST, B1, FRONT, B1, nc.scalar.copy)
+        add_bias(0, A)
+        quantize_w(LAST, N1)
+        multiply(LAST, 1, A)
+        quantize_x(LAST, B1)
         for i in range(PACK):
-            gather(2, i, *B2)
-        interleave_x(2, *B2)
-        scatter(0, 0)
-        add_bias(1, 0)
-        quantize_x(2, *B1)
-        quantize_x(2, *B2)
+            gather(LAST, i, B2, B2)
+        interleave_x(LAST, B2, B2, B2, nc.scalar.copy)
+        scatter(0, A)
+        add_bias(1, A)
+        quantize_x(LAST, B2)
         for m in range(M_TILES):
-            multiply(2, m, 1)
-        scatter(1, 0)
+            multiply(LAST, m, B)
+        scatter(1, A)
         for m in range(M_TILES):
-            add_bias(m, 1)
+            add_bias(m, B)
         for m in range(M_TILES):
-            scatter(m, 1)
+            scatter(m, B)
             nc.sync.dma_start(out=out[m * P : (m + 1) * P, :], in_=placed[m][:])

@@ -73,15 +73,13 @@ def tile_list_hboth_bias_kernel(tc, xT, w, wgt, b, wgo, offs, offs2, out):
         nc.sync.dma_start(out=wgt_sb[:, H:S], in_=wgt[:, H:S])
         for i in range(1, PACK):
             load_x(0, i)
-        load_x(1, 0)
-        load_x(1, 1)
-        load_w(0, ALL_N)
-        load_x(1, 2)
-        load_x(1, 3)
+        for i in range(PACK):
+            load_x(1, i)
         load_x(2, 0)
         load_x(2, 1)
-        load_w(1, ALL_N)
+        load_w(0, ALL_N)
         load_x(2, 2)
+        load_w(1, ALL_N)
         load_x(2, 3)
         load_w(2, ALL_N)
         load_b(0)
@@ -180,24 +178,24 @@ def tile_list_hboth_bias_kernel(tc, xT, w, wgt, b, wgo, offs, offs2, out):
         for i in range(2):
             gather(1, i, WHOLE, WHOLE)
         quantize_x(0, WHOLE)
-        interleave_w(0, ALL_N)
         gather(1, 2, WHOLE, WHOLE)
-        quantize_w(0, ALL_N)
-        multiply_pass(0)
         for part in (A, B):
             gather(1, 3, part, WHOLE)
             interleave_x(1, part, WHOLE, part, nc.scalar.copy)
         for i, part in enumerate((A, B)):
             gather(LAST, i, FRONT, FRONT)
             quantize_x(1, part)
-        interleave_w(1, ALL_N)
+        interleave_w(0, ALL_N)
         gather(LAST, 2, FRONT, FRONT)
-        quantize_w(1, ALL_N)
-        multiply_pass(1)
+        quantize_w(0, ALL_N)
+        multiply_pass(0)
+        interleave_w(1, ALL_N)
         gather(LAST, 3, A, FRONT)
         interleave_x(LAST, A1, FRONT, A, nc.scalar.copy)
         gather(LAST, 3, B1, FRONT)
         interleave_x(LAST, A2, FRONT, A, nc.vector.tensor_copy)
+        quantize_w(1, ALL_N)
+        multiply_pass(1)
         interleave_w(LAST, N0)
         quantize_x(LAST, A)
         quantize_w(LAST, N0)

@@ -67,18 +67,17 @@ def tile_list_hboth_bias_kernel(tc, xT, w, wgt, b, wgo, offs, offs2, out):
         def load_b(m):
             nc.sync.dma_start(out=b_sb[m][:], in_=b[m * P : (m + 1) * P].rearrange("(p o) -> p o", o=1))
 
+        wgt_cut = new_tile([P, 32], F32, "wgt_cut")
+        nc.sync.dma_start(out=wgt_cut[:], in_=wgt.rearrange("(g r) (s c) -> g r s c", r=16, c=32)[:, 0, :, :])
         nc.sync.dma_start(out=idx[:], in_=offs)
-        nc.sync.dma_start(out=wgt_sb[:, 0:H], in_=wgt[:, 0:H])
-        load_x(0, 0)
-        nc.sync.dma_start(out=wgt_sb[:, H:S], in_=wgt[:, H:S])
-        for i in range(1, PACK):
-            load_x(0, i)
         for i in range(PACK):
+            load_x(0, i)
+        for i in range(PACK - 1):
             load_x(1, i)
-        load_x(2, 0)
-        load_x(2, 1)
         load_w(0, ALL_N)
-        load_x(2, 2)
+        load_x(1, 3)
+        for i in range(PACK - 1):
+            load_x(2, i)
         load_w(1, ALL_N)
         load_x(2, 3)
         load_w(2, ALL_N)
@@ -88,8 +87,22 @@ def tile_list_hboth_bias_kernel(tc, xT, w, wgt, b, wgo, offs, offs2, out):
         load_b(1)
 
         placed = [new_tile([P, T], F32, f"placed{m}") for m in range(M_TILES)]
-        for m in range(M_TILES):
-            nc.vector.memset(placed[m][:], 0.0)
+        nc.vector.memset(placed[0][:], 0.0)
+        nc.gpsimd.memset(placed[1][:], 0.0)
+
+        wgt_turned = new_tile([P, 32], F32, "wgt_turned")
+        wgt_spread = new_tile([P, S], F32, "wgt_spread")
+        nc.vector.transpose(wgt_turned[:], wgt_cut[:])
+        for lo, hi in (A, B):
+            nc.vector.tensor_copy(
+                out=wgt_spread[:, lo:hi].rearrange("p (s h r) -> p s h r", h=2, r=16),
+                in_=wgt_turned[:]
+                .rearrange("p (h s) -> p s h", h=2)[:, lo // 32 : hi // 32, :]
+                .unsqueeze(3)
+                .to_broadcast([P, 8, 2, 16]),
+            )
+        for lo, hi in (A, B):
+            nc.vector.transpose(wgt_sb[:, lo:hi], wgt_spread[:, lo:hi])
 
         g_sb, x_bf, w_bf, acc, y_sb = {}, {}, {}, {}, {}
         x_codes = [new_tile([P, S], U32, f"xc{a}") for a in range(PASSES)]
@@ -179,16 +192,16 @@ def tile_list_hboth_bias_kernel(tc, xT, w, wgt, b, wgo, offs, offs2, out):
             gather(1, i, WHOLE, WHOLE)
         quantize_x(0, WHOLE)
         gather(1, 2, WHOLE, WHOLE)
+        interleave_w(0, ALL_N)
         for part in (A, B):
             gather(1, 3, part, WHOLE)
             interleave_x(1, part, WHOLE, part, nc.scalar.copy)
+        quantize_w(0, ALL_N)
+        multiply_pass(0)
         for i, part in enumerate((A, B)):
             gather(LAST, i, FRONT, FRONT)
             quantize_x(1, part)
-        interleave_w(0, ALL_N)
         gather(LAST, 2, FRONT, FRONT)
-        quantize_w(0, ALL_N)
-        multiply_pass(0)
         interleave_w(1, ALL_N)
         gather(LAST, 3, A, FRONT)
         interleave_x(LAST, A1, FRONT, A, nc.scalar.copy)

@@ -88,7 +88,7 @@ def tile_list_hboth_bias_kernel(tc, xT, w, wgt, b, wgo, offs, offs2, out):
 
         placed = [new_tile([P, T], F32, f"placed{m}") for m in range(M_TILES)]
         nc.vector.memset(placed[0][:], 0.0)
-        nc.gpsimd.memset(placed[1][:], 0.0)
+        nc.vector.memset(placed[1][:], 0.0)
 
         wgt_turned = new_tile([P, 32], F32, "wgt_turned")
         wgt_spread = new_tile([P, S], F32, "wgt_spread")

@@ -31,12 +31,10 @@ def tile_list_hboth_bias_kernel(tc, xT, w, wgt, b, wgo, offs, offs2, out):
         tc.psum_pool(name="psum", bufs=1) as psum,
     ):
         held = {
-            "wbf2_0": "late",
-            "g2_384": "late",
-            "y1_0": "late",
-            "xbf2_0": "parts",
-            "xbf2_256": "parts",
-            "xbf2_384": "parts",
+            "wbf2_0": "second",
+            "xbf2_384": "second",
+            "w2_0": "third",
+            "y0_0": "third",
         }
 
         def new_tile(shape, dtype, name):
@@ -44,7 +42,9 @@ def tile_list_hboth_bias_kernel(tc, xT, w, wgt, b, wgo, offs, offs2, out):
 
         WHOLE, A, B = (0, S), (0, H), (H, S)
         A1, A2, B1, B2 = (0, 128), (128, 256), (256, 384), (384, 512)
-        FRONT = (0, 384)
+        REST = (128, S)
+        MID = (128, 384)
+        BANKS = [(0, A1), (0, MID), (0, B2), (1, WHOLE)]
         ALL_N, N0, N1 = (0, M), (0, P), (P, M)
 
         idx = keep.tile([P, S // 16], U16, name="idx")
@@ -72,12 +72,12 @@ def tile_list_hboth_bias_kernel(tc, xT, w, wgt, b, wgo, offs, offs2, out):
         nc.sync.dma_start(out=idx[:], in_=offs)
         for i in range(PACK):
             load_x(0, i)
-        for i in range(PACK - 1):
+        for i in range(PACK):
             load_x(1, i)
+        load_x(2, 0)
+        load_x(2, 1)
         load_w(0, ALL_N)
-        load_x(1, 3)
-        for i in range(PACK - 1):
-            load_x(2, i)
+        load_x(2, 2)
         load_w(1, ALL_N)
         load_x(2, 3)
         load_w(2, ALL_N)
@@ -141,9 +141,9 @@ def tile_list_hboth_bias_kernel(tc, xT, w, wgt, b, wgo, offs, offs2, out):
                 in_=x_bf[a, part][:].rearrange("p j i -> p (j i)"),
             )
 
-        def interleave_w(a, ns):
+        def interleave_w(a, ns, copy=nc.scalar.copy):
             w_bf[a, ns] = new_tile([P, ns[1] - ns[0], PACK], BF16, f"wbf{a}_{ns[0]}")
-            weave(nc.scalar.copy, w_bf[a, ns][:], w_sb[a, ALL_N][:, :, ns[0] : ns[1]])
+            weave(copy, w_bf[a, ns][:], w_sb[a, ALL_N][:, :, ns[0] : ns[1]])
 
         def quantize_w(a, ns):
             nc.vector.quantize_mx(
@@ -167,13 +167,15 @@ def tile_list_hboth_bias_kernel(tc, xT, w, wgt, b, wgo, offs, offs2, out):
             )
 
         def multiply_pass(a):
-            for part in (A, B):
-                for m in range(M_TILES):
-                    multiply(a, m, part)
+            for m, part in BANKS:
+                multiply(a, m, part)
 
-        def add_bias(m, part):
-            y_sb[m, part] = new_tile([P, part[1] - part[0]], F32, f"y{m}_{part[0]}")
-            nc.scalar.activation(out=y_sb[m, part][:], in_=acc[m, part][:], func=IDENTITY, bias=b_sb[m][:])
+        def add_bias(m, part, into):
+            if (m, into) not in y_sb:
+                y_sb[m, into] = new_tile([P, into[1] - into[0]], F32, f"y{m}_{into[0]}")
+            nc.scalar.activation(
+                out=y_sb[m, into][:, within(part, into)], in_=acc[m, part][:], func=IDENTITY, bias=b_sb[m][:]
+            )
 
         def scatter(m, part):
             nc.vector.tensor_tensor(
@@ -192,44 +194,40 @@ def tile_list_hboth_bias_kernel(tc, xT, w, wgt, b, wgo, offs, offs2, out):
             gather(1, i, WHOLE, WHOLE)
         quantize_x(0, WHOLE)
         gather(1, 2, WHOLE, WHOLE)
-        interleave_w(0, ALL_N)
         for part in (A, B):
             gather(1, 3, part, WHOLE)
             interleave_x(1, part, WHOLE, part, nc.scalar.copy)
+        for i, part in enumerate((A, B)):
+            gather(LAST, i, WHOLE, WHOLE)
+            quantize_x(1, part)
+        interleave_w(0, ALL_N)
+        gather(LAST, 2, WHOLE, WHOLE)
         quantize_w(0, ALL_N)
         multiply_pass(0)
-        for i, part in enumerate((A, B)):
-            gather(LAST, i, FRONT, FRONT)
-            quantize_x(1, part)
-        gather(LAST, 2, FRONT, FRONT)
         interleave_w(1, ALL_N)
-        gather(LAST, 3, A, FRONT)
-        interleave_x(LAST, A1, FRONT, A, nc.scalar.copy)
-        gather(LAST, 3, B1, FRONT)
-        interleave_x(LAST, A2, FRONT, A, nc.vector.tensor_copy)
+        for part in (A1, MID):
+            gather(LAST, 3, part, WHOLE)
         quantize_w(1, ALL_N)
         multiply_pass(1)
-        interleave_w(LAST, N0)
-        quantize_x(LAST, A)
-        quantize_w(LAST, N0)
-        multiply(LAST, 0, A)
+        gather(LAST, 3, B2, WHOLE)
+        interleave_x(LAST, A1, WHOLE, A1, nc.scalar.copy)
+        interleave_x(LAST, MID, WHOLE, MID, nc.scalar.copy)
+        interleave_w(LAST, N0, nc.vector.tensor_copy)
         interleave_w(LAST, N1)
-        interleave_x(LAST, B1, FRONT, B1, nc.scalar.copy)
-        add_bias(0, A)
+        quantize_x(LAST, A1)
+        quantize_w(LAST, N0)
+        multiply(LAST, 0, A1)
+        interleave_x(LAST, B2, WHOLE, B2, nc.vector.tensor_copy)
+        for part in (MID, B2):
+            quantize_x(LAST, part)
         quantize_w(LAST, N1)
-        multiply(LAST, 1, A)
-        quantize_x(LAST, B1)
-        for i in range(PACK):
-            gather(LAST, i, B2, B2)
-        interleave_x(LAST, B2, B2, B2, nc.scalar.copy)
-        scatter(0, A)
-        add_bias(1, A)
-        quantize_x(LAST, B2)
-        for m in range(M_TILES):
-            multiply(LAST, m, B)
-        scatter(1, A)
-        for m in range(M_TILES):
-            add_bias(m, B)
-        for m in range(M_TILES):
-            scatter(m, B)
+        for m, part in BANKS[1:]:
+            multiply(LAST, m, part)
+        add_bias(0, A1, A1)
+        scatter(0, A1)
+        add_bias(0, MID, REST)
+        add_bias(0, B2, REST)
+        add_bias(1, WHOLE, WHOLE)
+        for m, part in enumerate((REST, WHOLE)):
+            scatter(m, part)
             nc.sync.dma_start(out=out[m * P : (m + 1) * P, :], in_=placed[m][:])

@@ -30,61 +30,61 @@ def tile_list_hboth_bias_kernel(tc, xT, w, wgt, b, wgo, offs, offs2, out):
         tc.tile_pool(name="keep", bufs=1) as keep,
         tc.psum_pool(name="psum", bufs=1) as psum,
     ):
-        held = {
-            "wbf2_0": "second",
-            "xbf2_384": "second",
-            "w2_0": "third",
-            "y0_0": "third",
-        }
+        held = {}
 
         def new_tile(shape, dtype, name):
             return keep.tile(shape, dtype, name=name, tag=held.get(name, name), align_bytes=64)
 
         WHOLE, A, B = (0, S), (0, H), (H, S)
         A1, A2, B1, B2 = (0, 128), (128, 256), (256, 384), (384, 512)
-        REST = (128, S)
-        MID = (128, 384)
-        BANKS = [(0, A1), (0, MID), (0, B2), (1, WHOLE)]
-        ALL_N, N0, N1 = (0, M), (0, P), (P, M)
+        BANKS = [(m, part) for part in (A1, A2, B) for m in range(M_TILES)]
 
         idx = keep.tile([P, S // 16], U16, name="idx")
         idx2 = keep.tile([P, S // 16], U16, name="idx2")
         wgt_sb = new_tile([P, S], F32, "wgt_sb")
         wgo_sb = new_tile([P, S], F32, "wgo_sb")
-        b_sb = [new_tile([P, 1], F32, f"b{m}") for m in range(M_TILES)]
+        wgt_cut = new_tile([P, 32], F32, "wgt_cut")
+        b_cut = new_tile([P, 32], F32, "b_cut")
+        b_turned = new_tile([P, 32], F32, "b_turned")
         x_sb = [[new_tile([P, T], F32, f"x{a}_{i}") for i in range(PACK)] for a in range(PASSES)]
-        w_sb = {}
+        g_flat = [new_tile([P, PACK * S + (H if a == LAST else 0)], F32, f"g{a}") for a in range(PASSES)]
+        g_sb = [g[:, 0 : PACK * S].rearrange("p (i j) -> p i j", i=PACK) for g in g_flat]
+        w_raw = {}
 
         def load_x(a, i):
             rows = xT[a * K_PASS : (a + 1) * K_PASS, :].rearrange("(p i) t -> p i t", i=PACK)
             nc.sync.dma_start(out=x_sb[a][i][:], in_=rows[:, i, :])
 
-        def load_w(a, ns):
-            w_sb[a, ns] = new_tile([P, PACK, ns[1] - ns[0]], F32, f"w{a}_{ns[0]}")
-            rows = w[a * K_PASS : (a + 1) * K_PASS, ns[0] : ns[1]].rearrange("(p i) n -> p i n", i=PACK)
-            nc.sync.dma_start(out=w_sb[a, ns][:], in_=rows)
+        def w_rows(a):
+            return w[a * K_PASS : (a + 1) * K_PASS, :].rearrange("(p i) n -> p i n", i=PACK)
 
-        def load_b(m):
-            nc.sync.dma_start(out=b_sb[m][:], in_=b[m * P : (m + 1) * P].rearrange("(p o) -> p o", o=1))
+        def load_w(a):
+            raw = new_tile([P, PACK, M], F32, f"w{a}")
+            nc.sync.dma_start(out=raw[:], in_=w_rows(a))
+            for m in range(M_TILES):
+                w_raw[a, m] = raw[:, :, m * P : (m + 1) * P]
 
-        wgt_cut = new_tile([P, 32], F32, "wgt_cut")
         nc.sync.dma_start(out=wgt_cut[:], in_=wgt.rearrange("(g r) (s c) -> g r s c", r=16, c=32)[:, 0, :, :])
+        nc.gpsimd.memset(b_cut[:], 0.0)
+        nc.sync.dma_start(out=b_cut[0:P:16, :], in_=b.rearrange("(m q c) -> q m c", m=M_TILES, c=32))
+        load_x(0, 0)
         nc.sync.dma_start(out=idx[:], in_=offs)
-        for i in range(PACK):
+        for i in range(1, PACK):
             load_x(0, i)
         for i in range(PACK):
             load_x(1, i)
         load_x(2, 0)
         load_x(2, 1)
-        load_w(0, ALL_N)
+        load_w(0)
         load_x(2, 2)
-        load_w(1, ALL_N)
+        load_w(1)
         load_x(2, 3)
-        load_w(2, ALL_N)
-        load_b(0)
+        w_raw[LAST, 0] = g_flat[LAST][:, PACK * S - H : PACK * S + H].rearrange("p (i n) -> p i n", i=PACK)
+        w_raw[LAST, 1] = new_tile([P, PACK, P], F32, "w_last")[:]
+        for m in range(M_TILES):
+            nc.sync.dma_start(out=w_raw[LAST, m], in_=w_rows(LAST)[:, :, m * P : (m + 1) * P])
         nc.sync.dma_start(out=idx2[:], in_=offs2)
         nc.sync.dma_start(out=wgo_sb[:], in_=wgo)
-        load_b(1)
 
         placed = [new_tile([P, T], F32, f"placed{m}") for m in range(M_TILES)]
         nc.vector.memset(placed[0][:], 0.0)
@@ -93,6 +93,7 @@ def tile_list_hboth_bias_kernel(tc, xT, w, wgt, b, wgo, offs, offs2, out):
         wgt_turned = new_tile([P, 32], F32, "wgt_turned")
         wgt_spread = new_tile([P, S], F32, "wgt_spread")
         nc.vector.transpose(wgt_turned[:], wgt_cut[:])
+        nc.vector.transpose(b_turned[:], b_cut[:])
         for lo, hi in (A, B):
             nc.vector.tensor_copy(
                 out=wgt_spread[:, lo:hi].rearrange("p (s h r) -> p s h r", h=2, r=16),
@@ -104,20 +105,25 @@ def tile_list_hboth_bias_kernel(tc, xT, w, wgt, b, wgo, offs, offs2, out):
         for lo, hi in (A, B):
             nc.vector.transpose(wgt_sb[:, lo:hi], wgt_spread[:, lo:hi])
 
-        g_sb, x_bf, w_bf, acc, y_sb = {}, {}, {}, {}, {}
+        x_bf, acc, y_sb = {}, {}, {}
         x_codes = [new_tile([P, S], U32, f"xc{a}") for a in range(PASSES)]
         x_scales = [new_tile([P, S], U8, f"xs{a}") for a in range(PASSES)]
-        w_codes = [new_tile([P, M], U32, f"wc{a}") for a in range(PASSES)]
-        w_scales = [new_tile([P, M], U8, f"ws{a}") for a in range(PASSES)]
+        W_ORDER = [(0, 0), (0, 1), (1, 0), (2, 0), (1, 1), (2, 1)]
+        W_CALLS = [W_ORDER[0:2], W_ORDER[2:3], W_ORDER[3:4], W_ORDER[4:6]]
+        w_bf, w_codes, w_scales, w_place = {}, {}, {}, {}
+        for c, blocks in enumerate(W_CALLS):
+            w_bf[c] = new_tile([P, len(blocks) * P, PACK], BF16, f"wbf{c}")
+            w_codes[c] = new_tile([P, len(blocks) * P], U32, f"wc{c}")
+            w_scales[c] = new_tile([P, len(blocks) * P], U8, f"ws{c}")
+            for n, block in enumerate(blocks):
+                w_place[block] = (c, slice(n * P, (n + 1) * P))
 
         def within(part, whole):
             return slice(part[0] - whole[0], part[1] - whole[0])
 
-        def gather(a, i, part, into):
-            if (a, into) not in g_sb:
-                g_sb[a, into] = new_tile([P, PACK, into[1] - into[0]], F32, f"g{a}_{into[0]}")
+        def gather(a, i, part):
             nc.vector.tensor_tensor(
-                g_sb[a, into][:, i, within(part, into)],
+                g_sb[a][:, i, part[0] : part[1]],
                 x_sb[a][i][:].indirect(idx[:, part[0] // 16 : part[1] // 16]),
                 wgt_sb[:, part[0] : part[1]],
                 MULT,
@@ -129,10 +135,10 @@ def tile_list_hboth_bias_kernel(tc, xT, w, wgt, b, wgo, offs, offs2, out):
                 in_=src.rearrange("p i (c r) -> p c i r", r=RUN),
             )
 
-        def interleave_x(a, part, source, into, copy):
+        def interleave_x(a, part, into, copy=nc.scalar.copy):
             if (a, into) not in x_bf:
                 x_bf[a, into] = new_tile([P, into[1] - into[0], PACK], BF16, f"xbf{a}_{into[0]}")
-            weave(copy, x_bf[a, into][:, within(part, into), :], g_sb[a, source][:, :, within(part, source)])
+            weave(copy, x_bf[a, into][:, within(part, into), :], g_sb[a][:, :, part[0] : part[1]])
 
         def quantize_x(a, part):
             nc.vector.quantize_mx(
@@ -141,40 +147,35 @@ def tile_list_hboth_bias_kernel(tc, xT, w, wgt, b, wgo, offs, offs2, out):
                 in_=x_bf[a, part][:].rearrange("p j i -> p (j i)"),
             )
 
-        def interleave_w(a, ns, copy=nc.scalar.copy):
-            w_bf[a, ns] = new_tile([P, ns[1] - ns[0], PACK], BF16, f"wbf{a}_{ns[0]}")
-            weave(copy, w_bf[a, ns][:], w_sb[a, ALL_N][:, :, ns[0] : ns[1]])
+        def interleave_w(a, m, copy=nc.scalar.copy):
+            c, cols = w_place[a, m]
+            weave(copy, w_bf[c][:, cols, :], w_raw[a, m])
 
-        def quantize_w(a, ns):
+        def quantize_w(c):
             nc.vector.quantize_mx(
-                out=w_codes[a][:, ns[0] : ns[1]].bitcast(FP8X4),
-                scales=w_scales[a][:, ns[0] : ns[1]],
-                in_=w_bf[a, ns][:].rearrange("p n i -> p (n i)"),
+                out=w_codes[c][:].bitcast(FP8X4),
+                scales=w_scales[c][:],
+                in_=w_bf[c][:].rearrange("p n i -> p (n i)"),
             )
 
         def multiply(a, m, part):
             if a == 0:
                 acc[m, part] = psum.tile([P, part[1] - part[0]], F32, name=f"acc{m}_{part[0]}")
-            ns = slice(m * P, (m + 1) * P)
+            c, cols = w_place[a, m]
             nc.tensor.matmul_mx(
                 out=acc[m, part][:],
-                lhsT=w_codes[a][:, ns].bitcast(FP8X4),
-                lhsT_scale=w_scales[a][:, ns],
+                lhsT=w_codes[c][:, cols].bitcast(FP8X4),
+                lhsT_scale=w_scales[c][:, cols],
                 rhs=x_codes[a][:, part[0] : part[1]].bitcast(FP8X4),
                 rhs_scale=x_scales[a][:, part[0] : part[1]],
                 start=(a == 0),
                 stop=(a == LAST),
             )
 
-        def multiply_pass(a):
-            for m, part in BANKS:
-                multiply(a, m, part)
-
-        def add_bias(m, part, into):
-            if (m, into) not in y_sb:
-                y_sb[m, into] = new_tile([P, into[1] - into[0]], F32, f"y{m}_{into[0]}")
+        def add_bias(m, part):
+            y_sb[m, part] = new_tile([P, part[1] - part[0]], F32, f"y{m}_{part[0]}")
             nc.scalar.activation(
-                out=y_sb[m, into][:, within(part, into)], in_=acc[m, part][:], func=IDENTITY, bias=b_sb[m][:]
+                out=y_sb[m, part][:], in_=acc[m, part][:], func=IDENTITY, bias=b_turned[:, 16 * m : 16 * m + 1]
             )
 
         def scatter(m, part):
@@ -185,49 +186,65 @@ def tile_list_hboth_bias_kernel(tc, xT, w, wgt, b, wgo, offs, offs2, out):
                 MULT,
             )
 
-        gather(0, 0, A, WHOLE)
-        gather(0, 0, B, WHOLE)
-        for i in range(1, PACK):
-            gather(0, i, WHOLE, WHOLE)
-        interleave_x(0, WHOLE, WHOLE, WHOLE, nc.scalar.copy)
-        for i in range(2):
-            gather(1, i, WHOLE, WHOLE)
-        quantize_x(0, WHOLE)
-        gather(1, 2, WHOLE, WHOLE)
-        for part in (A, B):
-            gather(1, 3, part, WHOLE)
-            interleave_x(1, part, WHOLE, part, nc.scalar.copy)
-        for i, part in enumerate((A, B)):
-            gather(LAST, i, WHOLE, WHOLE)
-            quantize_x(1, part)
-        interleave_w(0, ALL_N)
-        gather(LAST, 2, WHOLE, WHOLE)
-        quantize_w(0, ALL_N)
-        multiply_pass(0)
-        interleave_w(1, ALL_N)
-        for part in (A1, MID):
-            gather(LAST, 3, part, WHOLE)
-        quantize_w(1, ALL_N)
-        multiply_pass(1)
-        gather(LAST, 3, B2, WHOLE)
-        interleave_x(LAST, A1, WHOLE, A1, nc.scalar.copy)
-        interleave_x(LAST, MID, WHOLE, MID, nc.scalar.copy)
-        interleave_w(LAST, N0, nc.vector.tensor_copy)
-        interleave_w(LAST, N1)
-        quantize_x(LAST, A1)
-        quantize_w(LAST, N0)
-        multiply(LAST, 0, A1)
-        interleave_x(LAST, B2, WHOLE, B2, nc.vector.tensor_copy)
-        for part in (MID, B2):
-            quantize_x(LAST, part)
-        quantize_w(LAST, N1)
-        for m, part in BANKS[1:]:
-            multiply(LAST, m, part)
-        add_bias(0, A1, A1)
-        scatter(0, A1)
-        add_bias(0, MID, REST)
-        add_bias(0, B2, REST)
-        add_bias(1, WHOLE, WHOLE)
-        for m, part in enumerate((REST, WHOLE)):
-            scatter(m, part)
+        def store(m):
             nc.sync.dma_start(out=out[m * P : (m + 1) * P, :], in_=placed[m][:])
+
+        gather(0, 0, A)
+        gather(0, 0, B)
+        for i in range(1, PACK):
+            gather(0, i, WHOLE)
+        interleave_x(0, WHOLE, WHOLE)
+        for i in range(2):
+            gather(1, i, WHOLE)
+        quantize_x(0, WHOLE)
+        gather(1, 2, WHOLE)
+        for part in (A, B):
+            gather(1, 3, part)
+            interleave_x(1, part, part)
+        for i, part in enumerate((A, B)):
+            gather(LAST, i, WHOLE)
+            quantize_x(1, part)
+        interleave_w(0, 0)
+        interleave_w(0, 1)
+        gather(LAST, 2, WHOLE)
+        quantize_w(0)
+        for m, part in BANKS:
+            multiply(0, m, part)
+        interleave_w(1, 0)
+        interleave_w(1, 1)
+        quantize_w(1)
+        for part in (A1, A2, B):
+            multiply(1, 0, part)
+        for part in (A1, A2):
+            gather(LAST, 3, part)
+            interleave_x(LAST, part, part)
+        interleave_w(LAST, 0, nc.vector.tensor_copy)
+        quantize_x(LAST, A1)
+        quantize_w(2)
+        multiply(LAST, 0, A1)
+        gather(LAST, 3, B)
+        interleave_w(LAST, 1)
+        quantize_x(LAST, A2)
+        quantize_w(3)
+        multiply(1, 1, A1)
+        multiply(LAST, 1, A1)
+        multiply(LAST, 0, A2)
+        multiply(1, 1, A2)
+        multiply(LAST, 1, A2)
+        multiply(1, 1, B)
+        add_bias(0, A1)
+        scatter(0, A1)
+        interleave_x(LAST, B1, B)
+        add_bias(1, A1)
+        scatter(1, A1)
+        interleave_x(LAST, B2, B)
+        quantize_x(LAST, B)
+        for m in range(M_TILES):
+            multiply(LAST, m, B)
+        for m in range(M_TILES):
+            add_bias(m, A2)
+            scatter(m, A2)
+        for m in range(M_TILES):
+            add_bias(m, B)
+            scatter(m, B)
+            store(m)

@@ -37,7 +37,7 @@ def tile_list_hboth_bias_kernel(tc, xT, w, wgt, b, wgo, offs, offs2, out):
 
         WHOLE, A, B = (0, S), (0, H), (H, S)
         A1, A2, B1, B2 = (0, 128), (128, 256), (256, 384), (384, 512)
-        BANKS = [(m, part) for part in (A1, A2, B) for m in range(M_TILES)]
+        BANKS = [(0, A1), (0, A2), (0, B), (1, A), (1, B)]
 
         idx = keep.tile([P, S // 16], U16, name="idx")
         idx2 = keep.tile([P, S // 16], U16, name="idx2")
@@ -71,11 +71,12 @@ def tile_list_hboth_bias_kernel(tc, xT, w, wgt, b, wgo, offs, offs2, out):
         nc.sync.dma_start(out=idx[:], in_=offs)
         for i in range(1, PACK):
             load_x(0, i)
-        for i in range(PACK):
+        for i in range(PACK - 1):
             load_x(1, i)
+        load_w(0)
+        load_x(1, 3)
         load_x(2, 0)
         load_x(2, 1)
-        load_w(0)
         load_x(2, 2)
         load_w(1)
         load_x(2, 3)
@@ -108,8 +109,7 @@ def tile_list_hboth_bias_kernel(tc, xT, w, wgt, b, wgo, offs, offs2, out):
         x_bf, acc, y_sb = {}, {}, {}
         x_codes = [new_tile([P, S], U32, f"xc{a}") for a in range(PASSES)]
         x_scales = [new_tile([P, S], U8, f"xs{a}") for a in range(PASSES)]
-        W_ORDER = [(0, 0), (0, 1), (1, 0), (2, 0), (1, 1), (2, 1)]
-        W_CALLS = [W_ORDER[0:2], W_ORDER[2:3], W_ORDER[3:4], W_ORDER[4:6]]
+        W_CALLS = [[(0, 0), (0, 1)], [(1, 0)], [(1, 1)], [(2, 0)], [(2, 1)]]
         w_bf, w_codes, w_scales, w_place = {}, {}, {}, {}
         for c, blocks in enumerate(W_CALLS):
             w_bf[c] = new_tile([P, len(blocks) * P, PACK], BF16, f"wbf{c}")
@@ -198,18 +198,18 @@ def tile_list_hboth_bias_kernel(tc, xT, w, wgt, b, wgo, offs, offs2, out):
             gather(1, i, WHOLE)
         quantize_x(0, WHOLE)
         gather(1, 2, WHOLE)
+        interleave_w(0, 0)
+        interleave_w(0, 1)
         for part in (A, B):
             gather(1, 3, part)
             interleave_x(1, part, part)
-        for i, part in enumerate((A, B)):
-            gather(LAST, i, WHOLE)
-            quantize_x(1, part)
-        interleave_w(0, 0)
-        interleave_w(0, 1)
-        gather(LAST, 2, WHOLE)
         quantize_w(0)
         for m, part in BANKS:
             multiply(0, m, part)
+        for i, part in enumerate((A, B)):
+            gather(LAST, i, WHOLE)
+            quantize_x(1, part)
+        gather(LAST, 2, WHOLE)
         interleave_w(1, 0)
         interleave_w(1, 1)
         quantize_w(1)
@@ -218,33 +218,31 @@ def tile_list_hboth_bias_kernel(tc, xT, w, wgt, b, wgo, offs, offs2, out):
         for part in (A1, A2):
             gather(LAST, 3, part)
             interleave_x(LAST, part, part)
+        quantize_w(2)
+        for part in (A, B):
+            multiply(1, 1, part)
         interleave_w(LAST, 0, nc.vector.tensor_copy)
         quantize_x(LAST, A1)
-        quantize_w(2)
+        quantize_w(3)
         multiply(LAST, 0, A1)
         gather(LAST, 3, B)
         interleave_w(LAST, 1)
         quantize_x(LAST, A2)
-        quantize_w(3)
-        multiply(1, 1, A1)
-        multiply(LAST, 1, A1)
         multiply(LAST, 0, A2)
-        multiply(1, 1, A2)
-        multiply(LAST, 1, A2)
-        multiply(1, 1, B)
+        quantize_w(4)
+        multiply(LAST, 1, A)
         add_bias(0, A1)
         scatter(0, A1)
-        interleave_x(LAST, B1, B)
-        add_bias(1, A1)
-        scatter(1, A1)
-        interleave_x(LAST, B2, B)
-        quantize_x(LAST, B)
+        interleave_x(LAST, B1, B1)
+        quantize_x(LAST, B1)
+        add_bias(0, A2)
+        scatter(0, A2)
+        interleave_x(LAST, B2, B2)
+        quantize_x(LAST, B2)
+        add_bias(1, A)
+        scatter(1, A)
         for m in range(M_TILES):
             multiply(LAST, m, B)
-        for m in range(M_TILES):
-            add_bias(m, A2)
-            scatter(m, A2)
-        for m in range(M_TILES):
             add_bias(m, B)
             scatter(m, B)
             store(m)

@@ -4,6 +4,7 @@ K, M, T, S = 1536, 256, 1024, 512
 
 F32 = mybir.dt.float32
 BF16 = mybir.dt.bfloat16
+I32 = mybir.dt.int32
 U32 = mybir.dt.uint32
 U16 = mybir.dt.uint16
 U8 = mybir.dt.uint8
@@ -88,8 +89,8 @@ def tile_list_hboth_bias_kernel(tc, xT, w, wgt, b, wgo, offs, offs2, out):
         nc.sync.dma_start(out=wgo_sb[:], in_=wgo)
 
         placed = [new_tile([P, T], F32, f"placed{m}") for m in range(M_TILES)]
-        nc.vector.memset(placed[0][:], 0.0)
-        nc.vector.memset(placed[1][:], 0.0)
+        for m in range(M_TILES):
+            nc.vector.memset(placed[m][:].bitcast(I32), 0)
 
         wgt_turned = new_tile([P, 32], F32, "wgt_turned")
         wgt_spread = new_tile([P, S], F32, "wgt_spread")

@@ -66,12 +66,12 @@ def tile_list_hboth_bias_kernel(tc, xT, w, wgt, b, wgo, offs, offs2, out):
                 w_raw[a, m] = raw[:, :, m * P : (m + 1) * P]
 
         nc.sync.dma_start(out=wgt_cut[:], in_=wgt.rearrange("(g r) (s c) -> g r s c", r=16, c=32)[:, 0, :, :])
-        nc.gpsimd.memset(b_cut[:], 0.0)
-        nc.sync.dma_start(out=b_cut[0:P:16, :], in_=b.rearrange("(m q c) -> q m c", m=M_TILES, c=32))
         load_x(0, 0)
         nc.sync.dma_start(out=idx[:], in_=offs)
         for i in range(1, PACK):
             load_x(0, i)
+        nc.gpsimd.memset(b_cut[:], 0.0)
+        nc.sync.dma_start(out=b_cut[0:P:16, :], in_=b.rearrange("(m q c) -> q m c", m=M_TILES, c=32))
         for i in range(PACK - 1):
             load_x(1, i)
         load_w(0)
@@ -95,7 +95,6 @@ def tile_list_hboth_bias_kernel(tc, xT, w, wgt, b, wgo, offs, offs2, out):
         wgt_turned = new_tile([P, 32], F32, "wgt_turned")
         wgt_spread = new_tile([P, S], F32, "wgt_spread")
         nc.vector.transpose(wgt_turned[:], wgt_cut[:])
-        nc.vector.transpose(b_turned[:], b_cut[:])
         for lo, hi in (A, B):
             nc.vector.tensor_copy(
                 out=wgt_spread[:, lo:hi].rearrange("p (s h r) -> p s h r", h=2, r=16),
@@ -195,6 +194,7 @@ def tile_list_hboth_bias_kernel(tc, xT, w, wgt, b, wgo, offs, offs2, out):
         for i in range(1, PACK):
             gather(0, i, WHOLE)
         interleave_x(0, WHOLE, WHOLE)
+        nc.vector.transpose(b_turned[:], b_cut[:])
         for i in range(2):
             gather(1, i, WHOLE)
         quantize_x(0, WHOLE)

@@ -31,14 +31,16 @@ def tile_list_hboth_bias_kernel(tc, xT, w, wgt, b, wgo, offs, offs2, out):
         tc.tile_pool(name="keep", bufs=1) as keep,
         tc.psum_pool(name="psum", bufs=1) as psum,
     ):
-        held = {}
+        held = {"w1": "second", "xbf2_0": "second"}
 
         def new_tile(shape, dtype, name):
             return keep.tile(shape, dtype, name=name, tag=held.get(name, name), align_bytes=64)
 
         WHOLE, A, B = (0, S), (0, H), (H, S)
         A1, A2, B1, B2 = (0, 128), (128, 256), (256, 384), (384, 512)
-        BANKS = [(0, A1), (0, A2), (0, B), (1, A), (1, B)]
+        MID, REST = (128, 384), (128, S)
+        PARTS = (A1, MID, B2)
+        BANKS = [(m, part) for m in range(M_TILES) for part in PARTS]
 
         idx = keep.tile([P, S // 16], U16, name="idx")
         idx2 = keep.tile([P, S // 16], U16, name="idx2")
@@ -48,7 +50,7 @@ def tile_list_hboth_bias_kernel(tc, xT, w, wgt, b, wgo, offs, offs2, out):
         b_cut = new_tile([P, 32], F32, "b_cut")
         b_turned = new_tile([P, 32], F32, "b_turned")
         x_sb = [[new_tile([P, T], F32, f"x{a}_{i}") for i in range(PACK)] for a in range(PASSES)]
-        g_flat = [new_tile([P, PACK * S + (H if a == LAST else 0)], F32, f"g{a}") for a in range(PASSES)]
+        g_flat = [new_tile([P, PACK * S + (3 * P if a == LAST else 0)], F32, f"g{a}") for a in range(PASSES)]
         g_sb = [g[:, 0 : PACK * S].rearrange("p (i j) -> p i j", i=PACK) for g in g_flat]
         w_raw = {}
 
@@ -78,10 +80,10 @@ def tile_list_hboth_bias_kernel(tc, xT, w, wgt, b, wgo, offs, offs2, out):
         load_x(1, 3)
         load_x(2, 0)
         load_x(2, 1)
-        load_x(2, 2)
         load_w(1)
+        load_x(2, 2)
         load_x(2, 3)
-        w_raw[LAST, 0] = g_flat[LAST][:, PACK * S - H : PACK * S + H].rearrange("p (i n) -> p i n", i=PACK)
+        w_raw[LAST, 0] = g_flat[LAST][:, PACK * S - P : PACK * S + 3 * P].rearrange("p (i n) -> p i n", i=PACK)
         w_raw[LAST, 1] = new_tile([P, PACK, P], F32, "w_last")[:]
         for m in range(M_TILES):
             nc.sync.dma_start(out=w_raw[LAST, m], in_=w_rows(LAST)[:, :, m * P : (m + 1) * P])
@@ -109,7 +111,7 @@ def tile_list_hboth_bias_kernel(tc, xT, w, wgt, b, wgo, offs, offs2, out):
         x_bf, acc, y_sb = {}, {}, {}
         x_codes = [new_tile([P, S], U32, f"xc{a}") for a in range(PASSES)]
         x_scales = [new_tile([P, S], U8, f"xs{a}") for a in range(PASSES)]
-        W_CALLS = [[(0, 0), (0, 1)], [(1, 0)], [(1, 1)], [(2, 0)], [(2, 1)]]
+        W_CALLS = [[(0, 0), (0, 1)], [(1, 0), (1, 1)], [(2, 0)], [(2, 1)]]
         w_bf, w_codes, w_scales, w_place = {}, {}, {}, {}
         for c, blocks in enumerate(W_CALLS):
             w_bf[c] = new_tile([P, len(blocks) * P, PACK], BF16, f"wbf{c}")
@@ -135,16 +137,16 @@ def tile_list_hboth_bias_kernel(tc, xT, w, wgt, b, wgo, offs, offs2, out):
                 in_=src.rearrange("p i (c r) -> p c i r", r=RUN),
             )
 
-        def interleave_x(a, part, into, copy=nc.scalar.copy):
+        def interleave_x(a, part, into, planes=slice(0, PACK)):
             if (a, into) not in x_bf:
                 x_bf[a, into] = new_tile([P, into[1] - into[0], PACK], BF16, f"xbf{a}_{into[0]}")
-            weave(copy, x_bf[a, into][:, within(part, into), :], g_sb[a][:, :, part[0] : part[1]])
+            weave(nc.scalar.copy, x_bf[a, into][:, within(part, into), planes], g_sb[a][:, planes, part[0] : part[1]])
 
-        def quantize_x(a, part):
+        def quantize_x(a, part, out_of):
             nc.vector.quantize_mx(
                 out=x_codes[a][:, part[0] : part[1]].bitcast(FP8X4),
                 scales=x_scales[a][:, part[0] : part[1]],
-                in_=x_bf[a, part][:].rearrange("p j i -> p (j i)"),
+                in_=x_bf[a, out_of][:, within(part, out_of), :].rearrange("p j i -> p (j i)"),
             )
 
         def interleave_w(a, m, copy=nc.scalar.copy):
@@ -172,10 +174,14 @@ def tile_list_hboth_bias_kernel(tc, xT, w, wgt, b, wgo, offs, offs2, out):
                 stop=(a == LAST),
             )
 
-        def add_bias(m, part):
-            y_sb[m, part] = new_tile([P, part[1] - part[0]], F32, f"y{m}_{part[0]}")
+        def add_bias(m, part, into):
+            if (m, into) not in y_sb:
+                y_sb[m, into] = new_tile([P, into[1] - into[0]], F32, f"y{m}_{into[0]}")
             nc.scalar.activation(
-                out=y_sb[m, part][:], in_=acc[m, part][:], func=IDENTITY, bias=b_turned[:, 16 * m : 16 * m + 1]
+                out=y_sb[m, into][:, within(part, into)],
+                in_=acc[m, part][:],
+                func=IDENTITY,
+                bias=b_turned[:, 16 * m : 16 * m + 1],
             )
 
         def scatter(m, part):
@@ -197,7 +203,7 @@ def tile_list_hboth_bias_kernel(tc, xT, w, wgt, b, wgo, offs, offs2, out):
         nc.vector.transpose(b_turned[:], b_cut[:])
         for i in range(2):
             gather(1, i, WHOLE)
-        quantize_x(0, WHOLE)
+        quantize_x(0, WHOLE, WHOLE)
         gather(1, 2, WHOLE)
         interleave_w(0, 0)
         interleave_w(0, 1)
@@ -209,41 +215,38 @@ def tile_list_hboth_bias_kernel(tc, xT, w, wgt, b, wgo, offs, offs2, out):
             multiply(0, m, part)
         for i, part in enumerate((A, B)):
             gather(LAST, i, WHOLE)
-            quantize_x(1, part)
+            quantize_x(1, part, part)
+        first_pair, second_pair = slice(0, 2), slice(2, PACK)
         gather(LAST, 2, WHOLE)
         interleave_w(1, 0)
         interleave_w(1, 1)
         quantize_w(1)
-        for part in (A1, A2, B):
-            multiply(1, 0, part)
-        for part in (A1, A2):
+        for m, part in BANKS:
+            multiply(1, m, part)
+        interleave_x(LAST, WHOLE, WHOLE, first_pair)
+        for part in (A1, A2, B1):
             gather(LAST, 3, part)
-            interleave_x(LAST, part, part)
-        quantize_w(2)
-        for part in (A, B):
-            multiply(1, 1, part)
+            interleave_x(LAST, part, WHOLE, second_pair)
         interleave_w(LAST, 0, nc.vector.tensor_copy)
-        quantize_x(LAST, A1)
-        quantize_w(3)
+        quantize_x(LAST, A1, WHOLE)
+        quantize_w(2)
         multiply(LAST, 0, A1)
-        gather(LAST, 3, B)
+        gather(LAST, 3, B2)
         interleave_w(LAST, 1)
-        quantize_x(LAST, A2)
-        multiply(LAST, 0, A2)
-        quantize_w(4)
-        multiply(LAST, 1, A)
-        add_bias(0, A1)
-        scatter(0, A1)
-        interleave_x(LAST, B1, B1)
-        quantize_x(LAST, B1)
-        add_bias(0, A2)
-        scatter(0, A2)
-        interleave_x(LAST, B2, B2)
-        quantize_x(LAST, B2)
-        add_bias(1, A)
-        scatter(1, A)
+        interleave_x(LAST, B2, WHOLE, second_pair)
+        quantize_x(LAST, MID, WHOLE)
+        quantize_w(3)
+        multiply(LAST, 1, A1)
+        multiply(LAST, 0, MID)
+        quantize_x(LAST, B2, WHOLE)
+        multiply(LAST, 0, B2)
+        for part in PARTS[1:]:
+            multiply(LAST, 1, part)
         for m in range(M_TILES):
-            multiply(LAST, m, B)
-            add_bias(m, B)
-            scatter(m, B)
+            add_bias(m, A1, A1)
+            scatter(m, A1)
+        for m in range(M_TILES):
+            for part in PARTS[1:]:
+                add_bias(m, part, REST)
+            scatter(m, REST)
             store(m)

@@ -67,7 +67,7 @@ def tile_list_hboth_bias_kernel(tc, xT, w, wgt, b, wgo, offs, offs2, out):
             for m in range(M_TILES):
                 w_raw[a, m] = raw[:, :, m * P : (m + 1) * P]
 
-        nc.sync.dma_start(out=wgt_cut[:], in_=wgt.rearrange("(g r) (s c) -> g r s c", r=16, c=32)[:, 0, :, :])
+        nc.sync.dma_start(out=wgt_cut[:], in_=wgt.rearrange("r (h v c) -> (r h) v c", h=2, c=32)[0 : 2 * P : 17, :, :])
         load_x(0, 0)
         nc.sync.dma_start(out=idx[:], in_=offs)
         for i in range(1, PACK):
@@ -111,7 +111,7 @@ def tile_list_hboth_bias_kernel(tc, xT, w, wgt, b, wgo, offs, offs2, out):
         x_bf, acc, y_sb = {}, {}, {}
         x_codes = [new_tile([P, S], U32, f"xc{a}") for a in range(PASSES)]
         x_scales = [new_tile([P, S], U8, f"xs{a}") for a in range(PASSES)]
-        W_CALLS = [[(0, 0), (0, 1)], [(1, 0), (1, 1)], [(2, 0)], [(2, 1)]]
+        W_CALLS = [[(a, m)] for a in range(PASSES) for m in range(M_TILES)]
         w_bf, w_codes, w_scales, w_place = {}, {}, {}, {}
         for c, blocks in enumerate(W_CALLS):
             w_bf[c] = new_tile([P, len(blocks) * P, PACK], BF16, f"wbf{c}")
@@ -206,21 +206,23 @@ def tile_list_hboth_bias_kernel(tc, xT, w, wgt, b, wgo, offs, offs2, out):
         quantize_x(0, WHOLE, WHOLE)
         gather(1, 2, WHOLE)
         interleave_w(0, 0)
+        quantize_w(0)
         interleave_w(0, 1)
         for part in (A, B):
             gather(1, 3, part)
             interleave_x(1, part, part)
-        quantize_w(0)
+        quantize_w(1)
         for m, part in BANKS:
             multiply(0, m, part)
         for i, part in enumerate((A, B)):
             gather(LAST, i, WHOLE)
             quantize_x(1, part, part)
         first_pair, second_pair = slice(0, 2), slice(2, PACK)
-        gather(LAST, 2, WHOLE)
         interleave_w(1, 0)
+        quantize_w(2)
+        gather(LAST, 2, WHOLE)
         interleave_w(1, 1)
-        quantize_w(1)
+        quantize_w(3)
         for m, part in BANKS:
             multiply(1, m, part)
         interleave_x(LAST, WHOLE, WHOLE, first_pair)
@@ -229,13 +231,13 @@ def tile_list_hboth_bias_kernel(tc, xT, w, wgt, b, wgo, offs, offs2, out):
             interleave_x(LAST, part, WHOLE, second_pair)
         interleave_w(LAST, 0, nc.vector.tensor_copy)
         quantize_x(LAST, A1, WHOLE)
-        quantize_w(2)
+        quantize_w(4)
         multiply(LAST, 0, A1)
         gather(LAST, 3, B2)
         interleave_w(LAST, 1)
         interleave_x(LAST, B2, WHOLE, second_pair)
         quantize_x(LAST, MID, WHOLE)
-        quantize_w(3)
+        quantize_w(5)
         multiply(LAST, 1, A1)
         multiply(LAST, 0, MID)
         quantize_x(LAST, B2, WHOLE)

@@ -31,7 +31,7 @@ def tile_list_hboth_bias_kernel(tc, xT, w, wgt, b, wgo, offs, offs2, out):
         tc.tile_pool(name="keep", bufs=1) as keep,
         tc.psum_pool(name="psum", bufs=1) as psum,
     ):
-        held = {"w1": "second", "xbf2_0": "second"}
+        held = {"w1": "second", "xbf2_0": "second", "xc_first": "third", "y0_128": "third"}
 
         def new_tile(shape, dtype, name):
             return keep.tile(shape, dtype, name=name, tag=held.get(name, name), align_bytes=64)
@@ -120,6 +120,11 @@ def tile_list_hboth_bias_kernel(tc, xT, w, wgt, b, wgo, offs, offs2, out):
             for n, block in enumerate(blocks):
                 w_place[block] = (c, slice(n * P, (n + 1) * P))
 
+        first_codes = new_tile([P, P], U32, "xc_first")
+
+        def codes_of(a, part):
+            return first_codes[:] if (a, part) == (LAST, A1) else x_codes[a][:, part[0] : part[1]]
+
         def within(part, whole):
             return slice(part[0] - whole[0], part[1] - whole[0])
 
@@ -144,7 +149,7 @@ def tile_list_hboth_bias_kernel(tc, xT, w, wgt, b, wgo, offs, offs2, out):
 
         def quantize_x(a, part, out_of):
             nc.vector.quantize_mx(
-                out=x_codes[a][:, part[0] : part[1]].bitcast(FP8X4),
+                out=codes_of(a, part).bitcast(FP8X4),
                 scales=x_scales[a][:, part[0] : part[1]],
                 in_=x_bf[a, out_of][:, within(part, out_of), :].rearrange("p j i -> p (j i)"),
             )
@@ -161,16 +166,16 @@ def tile_list_hboth_bias_kernel(tc, xT, w, wgt, b, wgo, offs, offs2, out):
             )
 
         def multiply(a, m, part):
-            if a == 0:
+            if a == 1:
                 acc[m, part] = psum.tile([P, part[1] - part[0]], F32, name=f"acc{m}_{part[0]}")
             c, cols = w_place[a, m]
             nc.tensor.matmul_mx(
                 out=acc[m, part][:],
                 lhsT=w_codes[c][:, cols].bitcast(FP8X4),
                 lhsT_scale=w_scales[c][:, cols],
-                rhs=x_codes[a][:, part[0] : part[1]].bitcast(FP8X4),
+                rhs=codes_of(a, part).bitcast(FP8X4),
                 rhs_scale=x_scales[a][:, part[0] : part[1]],
-                start=(a == 0),
+                start=(a == 1),
                 stop=(a == LAST),
             )
 
@@ -212,8 +217,6 @@ def tile_list_hboth_bias_kernel(tc, xT, w, wgt, b, wgo, offs, offs2, out):
             gather(1, 3, part)
             interleave_x(1, part, part)
         quantize_w(1)
-        for m, part in BANKS:
-            multiply(0, m, part)
         for i, part in enumerate((A, B)):
             gather(LAST, i, WHOLE)
             quantize_x(1, part, part)
@@ -225,6 +228,7 @@ def tile_list_hboth_bias_kernel(tc, xT, w, wgt, b, wgo, offs, offs2, out):
         quantize_w(3)
         for m, part in BANKS:
             multiply(1, m, part)
+            multiply(0, m, part)
         interleave_x(LAST, WHOLE, WHOLE, first_pair)
         for part in (A1, A2, B1):
             gather(LAST, 3, part)

@@ -47,8 +47,7 @@ def tile_list_hboth_bias_kernel(tc, xT, w, wgt, b, wgo, offs, offs2, out):
         wgt_sb = new_tile([P, S], F32, "wgt_sb")
         wgo_sb = new_tile([P, S], F32, "wgo_sb")
         wgt_cut = new_tile([P, 32], F32, "wgt_cut")
-        b_cut = new_tile([P, 32], F32, "b_cut")
-        b_turned = new_tile([P, 32], F32, "b_turned")
+        b_cols = new_tile([P, M_TILES], F32, "b_cols")
         x_sb = [[new_tile([P, T], F32, f"x{a}_{i}") for i in range(PACK)] for a in range(PASSES)]
         g_flat = [new_tile([P, PACK * S + (3 * P if a == LAST else 0)], F32, f"g{a}") for a in range(PASSES)]
         g_sb = [g[:, 0 : PACK * S].rearrange("p (i j) -> p i j", i=PACK) for g in g_flat]
@@ -72,8 +71,6 @@ def tile_list_hboth_bias_kernel(tc, xT, w, wgt, b, wgo, offs, offs2, out):
         nc.sync.dma_start(out=idx[:], in_=offs)
         for i in range(1, PACK):
             load_x(0, i)
-        nc.gpsimd.memset(b_cut[:], 0.0)
-        nc.sync.dma_start(out=b_cut[0:P:16, :], in_=b.rearrange("(m q c) -> q m c", m=M_TILES, c=32))
         for i in range(PACK - 1):
             load_x(1, i)
         load_w(0)
@@ -88,7 +85,10 @@ def tile_list_hboth_bias_kernel(tc, xT, w, wgt, b, wgo, offs, offs2, out):
         for m in range(M_TILES):
             nc.sync.dma_start(out=w_raw[LAST, m], in_=w_rows(LAST)[:, :, m * P : (m + 1) * P])
         nc.sync.dma_start(out=idx2[:], in_=offs2)
-        nc.sync.dma_start(out=wgo_sb[:], in_=wgo)
+        nc.sync.dma_start(out=wgo_sb[:, 0:P], in_=wgo[:, 0:P])
+        with nc.allow_non_contiguous_dma(reason="one bias value a partition"):
+            nc.sync.dma_start(out=b_cols[:], in_=b.rearrange("(m p) -> p m", m=M_TILES))
+        nc.sync.dma_start(out=wgo_sb[:, P:S], in_=wgo[:, P:S])
 
         placed = [new_tile([P, T], F32, f"placed{m}") for m in range(M_TILES)]
         for m in range(M_TILES):
@@ -186,7 +186,7 @@ def tile_list_hboth_bias_kernel(tc, xT, w, wgt, b, wgo, offs, offs2, out):
                 out=y_sb[m, into][:, within(part, into)],
                 in_=acc[m, part][:],
                 func=IDENTITY,
-                bias=b_turned[:, 16 * m : 16 * m + 1],
+                bias=b_cols[:, m : m + 1],
             )
 
         def scatter(m, part):
@@ -205,7 +205,6 @@ def tile_list_hboth_bias_kernel(tc, xT, w, wgt, b, wgo, offs, offs2, out):
         for i in range(1, PACK):
             gather(0, i, WHOLE)
         interleave_x(0, WHOLE, WHOLE)
-        nc.vector.transpose(b_turned[:], b_cut[:])
         for i in range(2):
             gather(1, i, WHOLE)
         quantize_x(0, WHOLE, WHOLE)

import concourse.mybir as mybir

K, M, T, S = 1536, 256, 1024, 512

F32 = mybir.dt.float32
BF16 = mybir.dt.bfloat16
I32 = mybir.dt.int32
U32 = mybir.dt.uint32
U16 = mybir.dt.uint16
U8 = mybir.dt.uint8
FP8X4 = mybir.dt.float8_e4m3fn_x4
MULT = mybir.AluOpType.mult
IDENTITY = mybir.ActivationFunctionType.Identity

P = 128
PACK = 4
K_PASS = P * PACK
PASSES = K // K_PASS
LAST = PASSES - 1
M_TILES = M // P
H = S // 2
RUN = 4

FLOPS = 2 * K * M * S


def tile_list_hboth_bias_kernel(tc, xT, w, wgt, b, wgo, offs, offs2, out):
    nc = tc.nc

    with (
        tc.tile_pool(name="keep", bufs=1) as keep,
        tc.psum_pool(name="psum", bufs=1) as psum,
    ):
        held = {"w1": "second", "xbf2_0": "second", "xc_first": "third", "y0_128": "third"}

        def new_tile(shape, dtype, name):
            return keep.tile(shape, dtype, name=name, tag=held.get(name, name), align_bytes=64)

        WHOLE, A, B = (0, S), (0, H), (H, S)
        A1, A2, B1, B2 = (0, 128), (128, 256), (256, 384), (384, 512)
        MID, REST = (128, 384), (128, S)
        PARTS = (A1, MID, B2)
        BANKS = [(m, part) for m in range(M_TILES) for part in PARTS]

        idx = keep.tile([P, S // 16], U16, name="idx")
        idx2 = keep.tile([P, S // 16], U16, name="idx2")
        wgt_sb = new_tile([P, S], F32, "wgt_sb")
        wgo_sb = new_tile([P, S], F32, "wgo_sb")
        wgt_cut = new_tile([P, 32], F32, "wgt_cut")
        b_cols = new_tile([P, M_TILES], F32, "b_cols")
        x_sb = [[new_tile([P, T], F32, f"x{a}_{i}") for i in range(PACK)] for a in range(PASSES)]
        g_flat = [new_tile([P, PACK * S + (3 * P if a == LAST else 0)], F32, f"g{a}") for a in range(PASSES)]
        g_sb = [g[:, 0 : PACK * S].rearrange("p (i j) -> p i j", i=PACK) for g in g_flat]
        w_raw = {}

        def load_x(a, i):
            rows = xT[a * K_PASS : (a + 1) * K_PASS, :].rearrange("(p i) t -> p i t", i=PACK)
            nc.sync.dma_start(out=x_sb[a][i][:], in_=rows[:, i, :])

        def w_rows(a):
            return w[a * K_PASS : (a + 1) * K_PASS, :].rearrange("(p i) n -> p i n", i=PACK)

        def load_w(a):
            raw = new_tile([P, PACK, M], F32, f"w{a}")
            nc.sync.dma_start(out=raw[:], in_=w_rows(a))
            for m in range(M_TILES):
                w_raw[a, m] = raw[:, :, m * P : (m + 1) * P]

        nc.sync.dma_start(out=wgt_cut[:], in_=wgt.rearrange("r (h v c) -> (r h) v c", h=2, c=32)[0 : 2 * P : 17, :, :])
        load_x(0, 0)
        nc.sync.dma_start(out=idx[:], in_=offs)
        for i in range(1, PACK):
            load_x(0, i)
        for i in range(PACK - 1):
            load_x(1, i)
        load_w(0)
        load_x(1, 3)
        load_x(2, 0)
        load_x(2, 1)
        load_w(1)
        load_x(2, 2)
        load_x(2, 3)
        w_raw[LAST, 0] = g_flat[LAST][:, PACK * S - P : PACK * S + 3 * P].rearrange("p (i n) -> p i n", i=PACK)
        w_raw[LAST, 1] = new_tile([P, PACK, P], F32, "w_last")[:]
        for m in range(M_TILES):
            nc.sync.dma_start(out=w_raw[LAST, m], in_=w_rows(LAST)[:, :, m * P : (m + 1) * P])
        nc.sync.dma_start(out=idx2[:], in_=offs2)
        nc.sync.dma_start(out=wgo_sb[:, 0:P], in_=wgo[:, 0:P])
        with nc.allow_non_contiguous_dma(reason="one bias value a partition"):
            nc.sync.dma_start(out=b_cols[:], in_=b.rearrange("(m p) -> p m", m=M_TILES))
        nc.sync.dma_start(out=wgo_sb[:, P:S], in_=wgo[:, P:S])

        placed = [new_tile([P, T], F32, f"placed{m}") for m in range(M_TILES)]
        for m in range(M_TILES):
            nc.vector.memset(placed[m][:].bitcast(I32), 0)

        wgt_turned = new_tile([P, 32], F32, "wgt_turned")
        wgt_spread = new_tile([P, S], F32, "wgt_spread")
        nc.vector.transpose(wgt_turned[:], wgt_cut[:])
        for lo, hi in (A, B):
            nc.vector.tensor_copy(
                out=wgt_spread[:, lo:hi].rearrange("p (s h r) -> p s h r", h=2, r=16),
                in_=wgt_turned[:]
                .rearrange("p (h s) -> p s h", h=2)[:, lo // 32 : hi // 32, :]
                .unsqueeze(3)
                .to_broadcast([P, 8, 2, 16]),
            )
        for lo, hi in (A, B):
            nc.vector.transpose(wgt_sb[:, lo:hi], wgt_spread[:, lo:hi])

        x_bf, acc, y_sb = {}, {}, {}
        x_codes = [new_tile([P, S], U32, f"xc{a}") for a in range(PASSES)]
        x_scales = [new_tile([P, S], U8, f"xs{a}") for a in range(PASSES)]
        W_CALLS = [[(a, m)] for a in range(PASSES) for m in range(M_TILES)]
        w_bf, w_codes, w_scales, w_place = {}, {}, {}, {}
        for c, blocks in enumerate(W_CALLS):
            w_bf[c] = new_tile([P, len(blocks) * P, PACK], BF16, f"wbf{c}")
            w_codes[c] = new_tile([P, len(blocks) * P], U32, f"wc{c}")
            w_scales[c] = new_tile([P, len(blocks) * P], U8, f"ws{c}")
            for n, block in enumerate(blocks):
                w_place[block] = (c, slice(n * P, (n + 1) * P))

        first_codes = new_tile([P, P], U32, "xc_first")

        def codes_of(a, part):
            return first_codes[:] if (a, part) == (LAST, A1) else x_codes[a][:, part[0] : part[1]]

        def within(part, whole):
            return slice(part[0] - whole[0], part[1] - whole[0])

        def gather(a, i, part):
            nc.vector.tensor_tensor(
                g_sb[a][:, i, part[0] : part[1]],
                x_sb[a][i][:].indirect(idx[:, part[0] // 16 : part[1] // 16]),
                wgt_sb[:, part[0] : part[1]],
                MULT,
            )

        def weave(copy, dst, src):
            copy(
                out=dst.rearrange("p (c r) i -> p c i r", r=RUN),
                in_=src.rearrange("p i (c r) -> p c i r", r=RUN),
            )

        def interleave_x(a, part, into, planes=slice(0, PACK)):
            if (a, into) not in x_bf:
                x_bf[a, into] = new_tile([P, into[1] - into[0], PACK], BF16, f"xbf{a}_{into[0]}")
            weave(nc.scalar.copy, x_bf[a, into][:, within(part, into), planes], g_sb[a][:, planes, part[0] : part[1]])

        def quantize_x(a, part, out_of):
            nc.vector.quantize_mx(
                out=codes_of(a, part).bitcast(FP8X4),
                scales=x_scales[a][:, part[0] : part[1]],
                in_=x_bf[a, out_of][:, within(part, out_of), :].rearrange("p j i -> p (j i)"),
            )

        def interleave_w(a, m, copy=nc.scalar.copy):
            c, cols = w_place[a, m]
            weave(copy, w_bf[c][:, cols, :], w_raw[a, m])

        def quantize_w(c):
            nc.vector.quantize_mx(
                out=w_codes[c][:].bitcast(FP8X4),
                scales=w_scales[c][:],
                in_=w_bf[c][:].rearrange("p n i -> p (n i)"),
            )

        def multiply(a, m, part):
            if a == 1:
                acc[m, part] = psum.tile([P, part[1] - part[0]], F32, name=f"acc{m}_{part[0]}")
            c, cols = w_place[a, m]
            nc.tensor.matmul_mx(
                out=acc[m, part][:],
                lhsT=w_codes[c][:, cols].bitcast(FP8X4),
                lhsT_scale=w_scales[c][:, cols],
                rhs=codes_of(a, part).bitcast(FP8X4),
                rhs_scale=x_scales[a][:, part[0] : part[1]],
                start=(a == 1),
                stop=(a == LAST),
            )

        def add_bias(m, part, into):
            if (m, into) not in y_sb:
                y_sb[m, into] = new_tile([P, into[1] - into[0]], F32, f"y{m}_{into[0]}")
            nc.scalar.activation(
                out=y_sb[m, into][:, within(part, into)],
                in_=acc[m, part][:],
                func=IDENTITY,
                bias=b_cols[:, m : m + 1],
            )

        def scatter(m, part):
            nc.vector.tensor_tensor(
                placed[m][:].indirect(idx2[:, part[0] // 16 : part[1] // 16]),
                y_sb[m, part][:],
                wgo_sb[:, part[0] : part[1]],
                MULT,
            )

        def store(m):
            nc.sync.dma_start(out=out[m * P : (m + 1) * P, :], in_=placed[m][:])

        gather(0, 0, A)
        gather(0, 0, B)
        for i in range(1, PACK):
            gather(0, i, WHOLE)
        interleave_x(0, WHOLE, WHOLE)
        for i in range(2):
            gather(1, i, WHOLE)
        quantize_x(0, WHOLE, WHOLE)
        gather(1, 2, WHOLE)
        interleave_w(0, 0)
        quantize_w(0)
        interleave_w(0, 1)
        for part in (A, B):
            gather(1, 3, part)
            interleave_x(1, part, part)
        quantize_w(1)
        for i, part in enumerate((A, B)):
            gather(LAST, i, WHOLE)
            quantize_x(1, part, part)
        first_pair, second_pair = slice(0, 2), slice(2, PACK)
        interleave_w(1, 0)
        quantize_w(2)
        gather(LAST, 2, WHOLE)
        interleave_w(1, 1)
        quantize_w(3)
        for m, part in BANKS:
            multiply(1, m, part)
            multiply(0, m, part)
        interleave_x(LAST, WHOLE, WHOLE, first_pair)
        for part in (A1, A2, B1):
            gather(LAST, 3, part)
            interleave_x(LAST, part, WHOLE, second_pair)
        interleave_w(LAST, 0, nc.vector.tensor_copy)
        quantize_x(LAST, A1, WHOLE)
        quantize_w(4)
        multiply(LAST, 0, A1)
        gather(LAST, 3, B2)
        interleave_w(LAST, 1)
        interleave_x(LAST, B2, WHOLE, second_pair)
        quantize_x(LAST, MID, WHOLE)
        quantize_w(5)
        multiply(LAST, 1, A1)
        multiply(LAST, 0, MID)
        quantize_x(LAST, B2, WHOLE)
        multiply(LAST, 0, B2)
        for part in PARTS[1:]:
            multiply(LAST, 1, part)
        for m in range(M_TILES):
            add_bias(m, A1, A1)
            scatter(m, A1)
        for m in range(M_TILES):
            for part in PARTS[1:]:
                add_bias(m, part, REST)
            scatter(m, REST)
            store(m)
